import numpy as np
import ml_dtypes


def mxq(x, axis, fmt="e4m3"):
    dtype, down = {"e4m3": (ml_dtypes.float8_e4m3fn, 7), "e5m2": (ml_dtypes.float8_e5m2, 14)}[fmt]
    v = np.moveaxis(np.asarray(x, np.float32).astype(ml_dtypes.bfloat16).astype(np.float64), axis, -1)
    blocks = v.reshape(v.shape[:-1] + (-1, 32))
    amax = np.abs(blocks).max(-1, keepdims=True)
    byte = np.maximum(np.where(amax > 0, np.frexp(amax)[1] - 1 + 127, 0) - down, 1)
    scale = np.exp2(byte - 127.0)
    codes = (blocks / scale).astype(np.float32).astype(dtype).astype(np.float64)
    return np.moveaxis((codes * scale).reshape(v.shape), -1, axis)


WIDE = False


def mx_kscale(k, group=512):
    if not WIDE:
        return np.ones(k)
    levels = np.array([10, -10, 5, -5, 0])
    if group != 512:
        return np.exp2(np.random.permutation(np.resize(levels, k // group))).repeat(group)
    if k % 512:
        return np.exp2(np.random.permutation(np.resize(levels, k // 32))).repeat(32)
    a = np.empty((k // 512, 16))
    for p in range(k // 512):
        a[p, :8] = np.random.permutation(np.resize(levels, 8))
        for g in range(8):
            far = levels[np.abs(levels - a[p, g]) >= 10]
            a[p, g + 8] = far[np.random.randint(len(far))]
    return np.exp2(a.ravel()).repeat(32)


def f64(x):
    return np.asarray(x).astype(np.float64)


def striped(idx):
    return np.tile(np.asarray(idx).reshape(-1, 16).T, (8, 1)).astype(np.uint16)


def unstriped(offs):
    return offs[:16].T.reshape(-1).astype(np.int64)


H, KV, D, NQ, N = 4, 1, 256, 512, 512


def setup_inputs():
    n = np.random.standard_normal
    s = mx_kscale(D, 0)[:, None]
    u = mx_kscale(N)
    t = np.random.uniform(0.5, 2.0, N) * u
    v = n((KV, N, 128))
    v[:, :, 127] = 1.0
    return {
        "qT": (n((H, D, NQ)) * s * (0.70 / np.sqrt(D))).astype(np.float32),
        "kT": (n((KV, D, N)) / s).astype(np.float32),
        "t": t.reshape(N, 1).astype(np.float32),
        "v": (v / t[:, None]).astype(np.float32),
        "og": n((H, NQ, 128)).astype(np.float32),
    }


def reference(qT, kT, t, v, og):
    a = np.repeat(mxq(f64(kT), 1, "e4m3"), H // KV, 0).transpose(0, 2, 1) @ mxq(f64(qT), 1, "e4m3")
    p = np.exp(a)
    w = p * f64(t)
    y = mxq(w, 1, "e4m3").transpose(0, 2, 1) @ np.repeat(mxq(f64(v), 1, "e4m3"), H // KV, 0)
    y = y / (y[:, :, 127:128])
    y = y / (1.0 + np.exp(-f64(og)))
    return y

@@ -1,0 +1,279 @@
+from contextlib import ExitStack
+
+import concourse.mybir as mybir
+
+H, D, NQ, N, E = 4, 256, 512, 512, 128
+FLOPS = 2 * H * NQ * N * D + 2 * H * NQ * N * E
+
+F32 = mybir.dt.float32
+BF16 = mybir.dt.bfloat16
+U32 = mybir.dt.uint32
+U8 = mybir.dt.uint8
+FP8X4 = mybir.dt.float8_e4m3fn_x4
+ACT = mybir.ActivationFunctionType
+ALU = mybir.AluOpType
+
+P = 128
+R = 64
+PACK = 4
+C = 256
+UNITS = 8
+
+
+def tile_rows_gate_gqa_kernel(tc, qT, kT, t, v, og, out):
+    nc = tc.nc
+    with ExitStack() as ctx:
+        keep = ctx.enter_context(tc.tile_pool(name="keep", bufs=1))
+        ring = ctx.enter_context(tc.tile_pool(name="ring", bufs=3))
+        psum = ctx.enter_context(tc.psum_pool(name="psum", bufs=1))
+        ctx.enter_context(tc.manual_schedule())
+
+        t_raw = keep.tile([P, PACK], F32, name="t_raw")
+        k_raw = keep.tile([P, PACK, N], F32, name="k_raw")
+        v_raw = keep.tile([P, PACK, E], F32, name="v_raw")
+        q_raw = [keep.tile([P, PACK, C], F32, name="q_raw%d" % i) for i in range(2)]
+        q_late = keep.tile([P, PACK, NQ], F32, name="q_late")
+        q_src = [q_raw[0][:], q_raw[1][:], q_late[:, :, 0:C], q_late[:, :, C:NQ]]
+        og_raw = [keep.tile([P, 2, 2, C], F32, name="og_raw%d" % i) for i in range(2)]
+
+        def load_q(i):
+            pair, ch = divmod(i, 2)
+            src = qT[2 * pair : 2 * pair + 2, :, ch * C : (ch + 1) * C]
+            nc.sync.dma_start(out=q_raw[i][:], in_=src.rearrange("h (p j) q -> (h p) j q", j=PACK))
+
+        def load_og(pair):
+            src = og[2 * pair : 2 * pair + 2].rearrange("h (k p c) e -> p (h k) (c e)", k=2, c=2)
+            nc.sync.dma_start(out=og_raw[pair][:].rearrange("p h k x -> p (h k) x"), in_=src)
+
+        k_src = kT[0].rearrange("(p j) n -> p j n", j=PACK)
+        nc.sync.dma_start(out=t_raw[:], in_=t.rearrange("(p j) o -> p (j o)", j=PACK))
+        nc.sync.dma_start(out=k_raw[0:R], in_=k_src)
+        nc.scalar.dma_start(out=k_raw[R:P], in_=k_src)
+        load_q(0)
+        load_q(1)
+        nc.sync.dma_start(out=v_raw[:], in_=v[0].rearrange("(p j) e -> p j e", j=PACK))
+        load_og(0)
+        nc.sync.dma_start(out=q_late[:], in_=qT[2:4].rearrange("h (p j) q -> (h p) j q", j=PACK))
+        load_og(1)
+
+        t_abs = keep.tile([P, PACK], F32, name="t_abs")
+        t_pos2 = keep.tile([P, PACK], F32, name="t_pos2")
+        t_sign = keep.tile([P, PACK], F32, name="t_sign")
+        ln0 = keep.tile([P, PACK], F32, name="ln0")
+        inv0 = keep.tile([P, PACK], F32, name="inv0")
+        ratio = keep.tile([P, PACK], F32, name="ratio")
+        ln_t = keep.tile([P, PACK], F32, name="ln_t")
+        nc.vector.scalar_tensor_tensor(out=t_abs[:], in0=t_raw[:], scalar=-1.0, in1=t_raw[:], op0=ALU.mult, op1=ALU.max)
+        nc.vector.tensor_scalar(out=t_pos2[:], in0=t_raw[:], scalar1=0.0, scalar2=2.0, op0=ALU.is_ge, op1=ALU.mult)
+        nc.scalar.activation(out=ln0[:], in_=t_abs[:], func=ACT.Ln)
+        nc.vector.tensor_scalar(out=t_sign[:], in0=t_pos2[:], scalar1=-1.0, scalar2=None, op0=ALU.add)
+        nc.scalar.activation(out=inv0[:], in_=ln0[:], func=ACT.Exp, scale=-1.0)
+
+        k_bf = [keep.tile([P, 2, P, PACK], BF16, name="k_bf%d" % i, align_bytes=64) for i in range(2)]
+        k_codes = [keep.tile([P, 2 * P], U32, name="k_codes%d" % i, align_bytes=64) for i in range(2)]
+        k_scales = [keep.tile([P, 2 * P], U8, name="k_scales%d" % i, align_bytes=64) for i in range(2)]
+        q_bf = [keep.tile([P, C, PACK], BF16, name="q_bf%d" % i, align_bytes=64) for i in range(4)]
+        q_codes = [keep.tile([P, C], U32, name="q_codes%d" % i, align_bytes=64) for i in range(4)]
+        q_scales = [keep.tile([P, C], U8, name="q_scales%d" % i, align_bytes=64) for i in range(4)]
+        v_bf = keep.tile([P, E, PACK], BF16, name="v_bf", align_bytes=64)
+        v_codes = keep.tile([P, E], U32, name="v_codes", align_bytes=64)
+        v_scales = keep.tile([P, E], U8, name="v_scales", align_bytes=64)
+
+        def k_views(i):
+            src = k_raw[:].rearrange("p j (s r) -> p s j r", r=PACK)[:, :, :, 2 * i : 2 * i + 2]
+            return k_bf[i][:].rearrange("p r s j -> p s j r"), src
+
+        def quantize(codes, scales, grouped):
+            nc.vector.quantize_mx(out=codes.bitcast(FP8X4), scales=scales, in_=grouped)
+
+        def interleave(dst, src):
+            nc.vector.tensor_copy(
+                out=dst.rearrange("p (c i) j -> p c j i", i=4),
+                in_=src.rearrange("p j (c i) -> p c j i", i=4),
+            )
+
+        def quant_k(i):
+            quantize(k_codes[i][:], k_scales[i][:], k_bf[i][:].rearrange("p r s j -> p (r s j)"))
+
+        def inter_q(i, cols=slice(0, C)):
+            interleave(q_bf[i][:, cols, :], q_src[i][:, :, cols])
+
+        def quant_q(i, cols=slice(0, C)):
+            quantize(q_codes[i][:, cols], q_scales[i][:, cols], q_bf[i][:, cols, :].rearrange("p c j -> p (c j)"))
+
+        banks = {}
+
+        def unit_of(u):
+            pair, rest = divmod(u, 4)
+            ch, g = divmod(rest, 2)
+            return pair, ch, g
+
+        def score_calls(u, half):
+            pair, ch, g = unit_of(u)
+            bank = psum.tile([P, 2, C], F32, name="score%d" % g, tag="score%d" % g, bufs=3)
+            banks[u, half] = bank
+            rows = slice(R * g, R * g + R)
+            calls = []
+            for c in range(2):
+                for r in range(2):
+                    calls.append((bank, rows, half, r, 2 * pair + ch, c))
+            return calls
+
+        def score(call):
+            bank, rows, half, r, qi, c = call
+            toks = slice(r * P, (r + 1) * P)
+            cols = slice(c * P, (c + 1) * P)
+            nc.tensor.matmul_mx(
+                out=bank[:, r, cols],
+                lhsT=k_codes[half][rows, toks].bitcast(FP8X4),
+                lhsT_scale=k_scales[half][rows, toks],
+                rhs=q_codes[qi][rows, cols].bitcast(FP8X4),
+                rhs_scale=q_scales[qi][rows, cols],
+                start=True,
+                stop=True,
+            )
+
+        def scores(*halves):
+            lists = [score_calls(u, half) for u, half in halves if u < UNITS]
+            for group in zip(*lists):
+                for call in group:
+                    score(call)
+
+        w_rows, w_bf, w_codes, w_scales, y, recip, gate, th = {}, {}, {}, {}, {}, {}, {}, {}
+
+        def exps(u, half):
+            if half == 0:
+                w_rows[u] = ring.tile([P, PACK, C], BF16, name="w_rows", tag="w_rows")
+            for r in range(2):
+                nc.scalar.activation(
+                    out=w_rows[u][:, 2 * half + r, :].rearrange("x (c p) -> x c p", c=2),
+                    in_=banks[u, half][:, r, :].rearrange("x (p c) -> x c p", c=2),
+                    func=ACT.Exp,
+                    bias=ln_t[:, 2 * half + r : 2 * half + r + 1],
+                )
+
+        def w_tiles(u):
+            w_bf[u] = ring.tile([P, C, PACK], BF16, name="w_bf", tag="w_bf", align_bytes=64)
+            w_codes[u] = ring.tile([P, C], U32, name="w_codes", tag="w_codes", align_bytes=64)
+            w_scales[u] = ring.tile([P, C], U8, name="w_scales", tag="w_scales", align_bytes=64)
+            y[u] = psum.tile([P, 2, E], F32, name="y", tag="y", bufs=2)
+
+        def w_interleave(u, cols=slice(0, C)):
+            interleave(w_bf[u][:, cols, :], w_rows[u][:, :, cols])
+
+        def w_quant(u, cols=slice(0, C)):
+            quantize(w_codes[u][:, cols], w_scales[u][:, cols], w_bf[u][:, cols, :].rearrange("p c j -> p (c j)"))
+
+        def values(u, c):
+            cols = slice(c * P, (c + 1) * P)
+            nc.tensor.matmul_mx(
+                out=y[u][:, c, :],
+                lhsT=w_codes[u][:, cols].bitcast(FP8X4),
+                lhsT_scale=w_scales[u][:, cols],
+                rhs=v_codes[:].bitcast(FP8X4),
+                rhs_scale=v_scales[:],
+                start=True,
+                stop=True,
+            )
+
+        def tanh_pair(i):
+            pair, ch = divmod(i, 2)
+            th[i] = ring.tile([P, 2, C], F32, name="th", tag="th")
+            nc.scalar.activation(out=th[i][:], in_=og_raw[pair][:, :, ch, :], func=ACT.Tanh, scale=0.5)
+
+        def gate_pair(i):
+            gate[i] = ring.tile([P, 2, C], F32, name="gate", tag="gate")
+            if i < 3:
+                nc.vector.tensor_scalar(out=gate[i][:], in0=th[i][:], scalar1=0.5, scalar2=0.5, op0=ALU.mult, op1=ALU.add)
+            else:
+                nc.scalar.activation(out=gate[i][:], in_=th[i][:], func=ACT.Copy, scale=0.5, bias=0.5)
+
+        def reciprocal(u):
+            recip[u] = ring.tile([P, 2], F32, name="recip", tag="recip")
+            nc.vector.reciprocal(out=recip[u][:], in_=y[u][:, :, E - 1])
+
+        def finish(u):
+            pair, ch, g = unit_of(u)
+            res = ring.tile([P, 2, E], F32, name="res", tag="res")
+            for c in range(2):
+                nc.vector.scalar_tensor_tensor(
+                    out=res[:, c, :],
+                    in0=y[u][:, c, :],
+                    scalar=recip[u][:, c : c + 1],
+                    in1=gate[u // 2][:, g, c * E : (c + 1) * E],
+                    op0=ALU.mult,
+                    op1=ALU.mult,
+                )
+            dst = out[2 * pair + g, ch * C : (ch + 1) * C, :].rearrange("(p c) e -> p c e", c=2)
+            nc.sync.dma_start(out=dst, in_=res[:])
+
+        dst, src = k_views(0)
+        nc.vector.tensor_copy(out=dst, in_=src)
+        dst, src = k_views(1)
+        nc.scalar.copy(out=dst, in_=src)
+        nc.vector.tensor_tensor(out=ratio[:], in0=inv0[:], in1=t_abs[:], op=ALU.mult)
+        quant_k(0)
+        nc.vector.scalar_tensor_tensor(out=ln_t[:], in0=ratio[:], scalar=-1.0, in1=ln0[:], op0=ALU.add, op1=ALU.add)
+        lo, hi = slice(0, P), slice(P, C)
+        inter_q(0, lo)
+        inter_q(0, hi)
+        quant_q(0, lo)
+        quant_q(0, hi)
+        scores((0, 0))
+        quant_k(1)
+        scores((0, 1), (1, 0))
+        scores((1, 1))
+        inter_q(1)
+        nc.vector.tensor_tensor(
+            out=v_bf[:].rearrange("p (c i) j -> p c j i", i=4),
+            in0=v_raw[:].rearrange("p j (c i) -> p c j i", i=4),
+            in1=t_sign[:].unsqueeze(1).unsqueeze(3).to_broadcast([P, E // 4, PACK, 4]),
+            op=ALU.mult,
+        )
+        quant_q(1)
+        quantize(v_codes[:], v_scales[:], v_bf[:].rearrange("p c j -> p (c j)"))
+        scores((2, 0))
+
+        last = UNITS - 1
+        for u in range(last):
+            exps(u, 0)
+            if u == 1:
+                scores((3, 1))
+            elif u == 2:
+                scores((4, 0))
+                scores((4, 1), (5, 0))
+            else:
+                scores((u + 2, 1), (u + 3, 0))
+            exps(u, 1)
+            if u in (1, 2, 4):
+                tanh_pair((1, 2, 4).index(u))
+            w_tiles(u)
+            w_interleave(u)
+            if u >= 1:
+                reciprocal(u - 1)
+            if u in (1, 2):
+                inter_q(1 + u)
+            if u in (1, 3, 5):
+                gate_pair(u // 2)
+            w_quant(u)
+            values(u, 0)
+            values(u, 1)
+            if u in (1, 2):
+                quant_q(1 + u)
+            if u >= 1:
+                finish(u - 1)
+        exps(last, 0)
+        exps(last, 1)
+        tanh_pair(3)
+        gate_pair(3)
+        w_tiles(last)
+        w_interleave(last, lo)
+        w_interleave(last, hi)
+        w_quant(last, lo)
+        values(last, 0)
+        w_quant(last, hi)
+        values(last, 1)
+        reciprocal(last - 1)
+        finish(last - 1)
+        reciprocal(last)
+        finish(last)

@@ -9,6 +9,7 @@ F32 = mybir.dt.float32
 BF16 = mybir.dt.bfloat16
 U32 = mybir.dt.uint32
 U8 = mybir.dt.uint8
+I32 = mybir.dt.int32
 FP8X4 = mybir.dt.float8_e4m3fn_x4
 ACT = mybir.ActivationFunctionType
 ALU = mybir.AluOpType
@@ -29,32 +30,31 @@ def tile_rows_gate_gqa_kernel(tc, qT, kT, t, v, og, out):
         ctx.enter_context(tc.manual_schedule())
 
         t_raw = keep.tile([P, PACK], F32, name="t_raw")
-        k_raw = keep.tile([P, PACK, N], F32, name="k_raw")
+        k_raw = keep.tile([P, PACK, C], F32, name="k_raw")
         v_raw = keep.tile([P, PACK, E], F32, name="v_raw")
-        q_raw = [keep.tile([P, PACK, C], F32, name="q_raw%d" % i) for i in range(2)]
-        q_late = keep.tile([P, PACK, NQ], F32, name="q_late")
-        q_src = [q_raw[0][:], q_raw[1][:], q_late[:, :, 0:C], q_late[:, :, C:NQ]]
+        q_raw = [keep.tile([P, PACK, NQ], F32, name="q_raw%d" % i) for i in range(2)]
         og_raw = [keep.tile([P, 2, 2, C], F32, name="og_raw%d" % i) for i in range(2)]
 
-        def load_q(i):
-            pair, ch = divmod(i, 2)
-            src = qT[2 * pair : 2 * pair + 2, :, ch * C : (ch + 1) * C]
-            nc.sync.dma_start(out=q_raw[i][:], in_=src.rearrange("h (p j) q -> (h p) j q", j=PACK))
+        def load_q(pair):
+            src = qT[2 * pair : 2 * pair + 2]
+            nc.sync.dma_start(out=q_raw[pair][:], in_=src.rearrange("h (p j) q -> (h p) j q", j=PACK))
 
         def load_og(pair):
-            src = og[2 * pair : 2 * pair + 2].rearrange("h (k p c) e -> p (h k) (c e)", k=2, c=2)
-            nc.sync.dma_start(out=og_raw[pair][:].rearrange("p h k x -> p (h k) x"), in_=src)
+            src = og[2 * pair : 2 * pair + 2].rearrange("h (p c) e -> p h (c e)", c=4)
+            nc.sync.dma_start(out=og_raw[pair][:].rearrange("p h k x -> p h (k x)"), in_=src)
 
         k_src = kT[0].rearrange("(p j) n -> p j n", j=PACK)
         nc.sync.dma_start(out=t_raw[:], in_=t.rearrange("(p j) o -> p (j o)", j=PACK))
-        nc.sync.dma_start(out=k_raw[0:R], in_=k_src)
-        nc.scalar.dma_start(out=k_raw[R:P], in_=k_src)
+        nc.sync.dma_start(out=k_raw[0:R], in_=k_src[:, :, 0:C])
+        nc.scalar.dma_start(out=k_raw[R:P], in_=k_src[:, :, C:N])
         load_q(0)
-        load_q(1)
         nc.sync.dma_start(out=v_raw[:], in_=v[0].rearrange("(p j) e -> p j e", j=PACK))
-        load_og(0)
-        nc.sync.dma_start(out=q_late[:], in_=qT[2:4].rearrange("h (p j) q -> (h p) j q", j=PACK))
-        load_og(1)
+
+        k_bf = keep.tile([P, PACK, R, PACK], BF16, name="k_bf", align_bytes=64)
+        k_codes = [keep.tile([P, PACK, P], U32, name="k_codes%d" % i, align_bytes=64) for i in range(2)]
+        k_scales = [keep.tile([P, PACK, P], U8, name="k_scales%d" % i, align_bytes=64) for i in range(2)]
+        for i in range(2):
+            nc.vector.memset(k_scales[i][:].rearrange("p r s -> p (r s)").bitcast(I32), 0)
 
         t_abs = keep.tile([P, PACK], F32, name="t_abs")
         t_pos2 = keep.tile([P, PACK], F32, name="t_pos2")
@@ -69,19 +69,12 @@ def tile_rows_gate_gqa_kernel(tc, qT, kT, t, v, og, out):
         nc.vector.tensor_scalar(out=t_sign[:], in0=t_pos2[:], scalar1=-1.0, scalar2=None, op0=ALU.add)
         nc.scalar.activation(out=inv0[:], in_=ln0[:], func=ACT.Exp, scale=-1.0)
 
-        k_bf = [keep.tile([P, 2, P, PACK], BF16, name="k_bf%d" % i, align_bytes=64) for i in range(2)]
-        k_codes = [keep.tile([P, 2 * P], U32, name="k_codes%d" % i, align_bytes=64) for i in range(2)]
-        k_scales = [keep.tile([P, 2 * P], U8, name="k_scales%d" % i, align_bytes=64) for i in range(2)]
         q_bf = [keep.tile([P, C, PACK], BF16, name="q_bf%d" % i, align_bytes=64) for i in range(4)]
         q_codes = [keep.tile([P, C], U32, name="q_codes%d" % i, align_bytes=64) for i in range(4)]
         q_scales = [keep.tile([P, C], U8, name="q_scales%d" % i, align_bytes=64) for i in range(4)]
         v_bf = keep.tile([P, E, PACK], BF16, name="v_bf", align_bytes=64)
         v_codes = keep.tile([P, E], U32, name="v_codes", align_bytes=64)
         v_scales = keep.tile([P, E], U8, name="v_scales", align_bytes=64)
-
-        def k_views(i):
-            src = k_raw[:].rearrange("p j (s r) -> p s j r", r=PACK)[:, :, :, 2 * i : 2 * i + 2]
-            return k_bf[i][:].rearrange("p r s j -> p s j r"), src
 
         def quantize(codes, scales, grouped):
             nc.vector.quantize_mx(out=codes.bitcast(FP8X4), scales=scales, in_=grouped)
@@ -92,11 +85,19 @@ def tile_rows_gate_gqa_kernel(tc, qT, kT, t, v, og, out):
                 in_=src.rearrange("p j (c i) -> p c j i", i=4),
             )
 
-        def quant_k(i):
-            quantize(k_codes[i][:], k_scales[i][:], k_bf[i][:].rearrange("p r s j -> p (r s j)"))
+        def q_views(i):
+            pair, ch = divmod(i, 2)
+            src = q_raw[pair][:].rearrange("p j (s c) -> p s j c", c=4)[:, :, :, 2 * ch : 2 * ch + 2]
+            return q_bf[i][:].rearrange("p (c s) j -> p s j c", c=2), src
 
-        def inter_q(i, cols=slice(0, C)):
-            interleave(q_bf[i][:, cols, :], q_src[i][:, :, cols])
+        def inter_q(i):
+            dst, src = q_views(i)
+            nc.vector.tensor_copy(out=dst, in_=src)
+
+        def k_window(g, rows, half):
+            codes = k_codes[g][rows, :, half * R : (half + 1) * R].bitcast(I32)
+            scales = k_scales[g][rows, :, half * R : (half + 1) * R].bitcast(I32)
+            return codes, scales
 
         def quant_q(i, cols=slice(0, C)):
             quantize(q_codes[i][:, cols], q_scales[i][:, cols], q_bf[i][:, cols, :].rearrange("p c j -> p (c j)"))
@@ -116,17 +117,16 @@ def tile_rows_gate_gqa_kernel(tc, qT, kT, t, v, og, out):
             calls = []
             for c in range(2):
                 for r in range(2):
-                    calls.append((bank, rows, half, r, 2 * pair + ch, c))
+                    calls.append((bank, g, rows, half, r, 2 * pair + ch, c))
             return calls
 
         def score(call):
-            bank, rows, half, r, qi, c = call
-            toks = slice(r * P, (r + 1) * P)
+            bank, g, rows, half, r, qi, c = call
             cols = slice(c * P, (c + 1) * P)
             nc.tensor.matmul_mx(
                 out=bank[:, r, cols],
-                lhsT=k_codes[half][rows, toks].bitcast(FP8X4),
-                lhsT_scale=k_scales[half][rows, toks],
+                lhsT=k_codes[g][rows, 2 * half + r, :].bitcast(FP8X4),
+                lhsT_scale=k_scales[g][rows, 2 * half + r, :],
                 rhs=q_codes[qi][rows, cols].bitcast(FP8X4),
                 rhs_scale=q_scales[qi][rows, cols],
                 start=True,
@@ -146,8 +146,8 @@ def tile_rows_gate_gqa_kernel(tc, qT, kT, t, v, og, out):
                 w_rows[u] = ring.tile([P, PACK, C], BF16, name="w_rows", tag="w_rows")
             for r in range(2):
                 nc.scalar.activation(
-                    out=w_rows[u][:, 2 * half + r, :].rearrange("x (c p) -> x c p", c=2),
-                    in_=banks[u, half][:, r, :].rearrange("x (p c) -> x c p", c=2),
+                    out=w_rows[u][:, 2 * half + r, :],
+                    in_=banks[u, half][:, r, :],
                     func=ACT.Exp,
                     bias=ln_t[:, 2 * half + r : 2 * half + r + 1],
                 )
@@ -204,26 +204,34 @@ def tile_rows_gate_gqa_kernel(tc, qT, kT, t, v, og, out):
                     op0=ALU.mult,
                     op1=ALU.mult,
                 )
-            dst = out[2 * pair + g, ch * C : (ch + 1) * C, :].rearrange("(p c) e -> p c e", c=2)
+            dst = out[2 * pair + g].rearrange("(p c) e -> p c e", c=4)[:, 2 * ch : 2 * ch + 2, :]
             nc.sync.dma_start(out=dst, in_=res[:])
 
-        dst, src = k_views(0)
-        nc.vector.tensor_copy(out=dst, in_=src)
-        dst, src = k_views(1)
-        nc.scalar.copy(out=dst, in_=src)
-        nc.vector.tensor_tensor(out=ratio[:], in0=inv0[:], in1=t_abs[:], op=ALU.mult)
-        quant_k(0)
-        nc.vector.scalar_tensor_tensor(out=ln_t[:], in0=ratio[:], scalar=-1.0, in1=ln0[:], op0=ALU.add, op1=ALU.add)
         lo, hi = slice(0, P), slice(P, C)
-        inter_q(0, lo)
-        inter_q(0, hi)
-        quant_q(0, lo)
-        quant_q(0, hi)
+        top, bottom = slice(0, R), slice(R, P)
+        nc.vector.tensor_copy(
+            out=k_bf[:].rearrange("p r s j -> p s j r"),
+            in_=k_raw[:].rearrange("p j (s r) -> p s j r", r=PACK),
+        )
+        nc.vector.tensor_tensor(out=ratio[:], in0=inv0[:], in1=t_abs[:], op=ALU.mult)
+        for r in range(PACK):
+            quantize(k_codes[0][:, r, 0:R], k_scales[0][:, r, 0:R], k_bf[:, r].rearrange("p s j -> p (s j)"))
+        for dst, src in zip(k_window(0, top, 1), k_window(0, bottom, 0)):
+            nc.sync.dma_start(out=dst, in_=src)
+        for dst, src in zip(k_window(1, bottom, 0), k_window(0, top, 0)):
+            nc.sync.dma_start(out=dst, in_=src)
+        load_q(1)
+        load_og(0)
+        load_og(1)
+        nc.vector.scalar_tensor_tensor(out=ln_t[:], in0=ratio[:], scalar=-1.0, in1=ln0[:], op0=ALU.add, op1=ALU.add)
+        inter_q(0)
+        dst, src = q_views(1)
+        nc.scalar.copy(out=dst, in_=src)
+        for dst, src in zip(k_window(1, bottom, 1), k_window(0, bottom, 0)):
+            nc.vector.tensor_copy(out=dst, in_=src)
+        quant_q(0)
         scores((0, 0))
-        quant_k(1)
         scores((0, 1), (1, 0))
-        scores((1, 1))
-        inter_q(1)
         nc.vector.tensor_tensor(
             out=v_bf[:].rearrange("p (c i) j -> p c j i", i=4),
             in0=v_raw[:].rearrange("p j (c i) -> p c j i", i=4),
@@ -232,18 +240,13 @@ def tile_rows_gate_gqa_kernel(tc, qT, kT, t, v, og, out):
         )
         quant_q(1)
         quantize(v_codes[:], v_scales[:], v_bf[:].rearrange("p c j -> p (c j)"))
-        scores((2, 0))
+        scores((1, 1), (2, 0))
+        inter_q(2)
 
         last = UNITS - 1
         for u in range(last):
             exps(u, 0)
-            if u == 1:
-                scores((3, 1))
-            elif u == 2:
-                scores((4, 0))
-                scores((4, 1), (5, 0))
-            else:
-                scores((u + 2, 1), (u + 3, 0))
+            scores((u + 2, 1), (u + 3, 0))
             exps(u, 1)
             if u in (1, 2, 4):
                 tanh_pair((1, 2, 4).index(u))
@@ -251,15 +254,15 @@ def tile_rows_gate_gqa_kernel(tc, qT, kT, t, v, og, out):
             w_interleave(u)
             if u >= 1:
                 reciprocal(u - 1)
-            if u in (1, 2):
-                inter_q(1 + u)
+            if u == 2:
+                inter_q(3)
             if u in (1, 3, 5):
                 gate_pair(u // 2)
             w_quant(u)
             values(u, 0)
             values(u, 1)
-            if u in (1, 2):
-                quant_q(1 + u)
+            if u in (0, 2):
+                quant_q(2 + u // 2)
             if u >= 1:
                 finish(u - 1)
         exps(last, 0)

@@ -49,6 +49,9 @@ def tile_rows_gate_gqa_kernel(tc, qT, kT, t, v, og, out):
         nc.scalar.dma_start(out=k_raw[R:P], in_=k_src[:, :, C:N])
         load_q(0)
         nc.sync.dma_start(out=v_raw[:], in_=v[0].rearrange("(p j) e -> p j e", j=PACK))
+        load_q(1)
+        load_og(0)
+        load_og(1)
 
         k_bf = keep.tile([P, PACK, R, PACK], BF16, name="k_bf", align_bytes=64)
         k_codes = [keep.tile([P, PACK, P], U32, name="k_codes%d" % i, align_bytes=64) for i in range(2)]
@@ -139,15 +142,19 @@ def tile_rows_gate_gqa_kernel(tc, qT, kT, t, v, og, out):
                 for call in group:
                     score(call)
 
-        w_rows, w_bf, w_codes, w_scales, y, recip, gate, th = {}, {}, {}, {}, {}, {}, {}, {}
+        w_rows, w_bf, w_codes, w_scales, y = {}, {}, {}, {}, {}
+        th = [keep.tile([P, 2, C], F32, name="th%d" % i) for i in range(4)]
+        gate = [keep.tile([P, 2, C], F32, name="gate%d" % i) for i in range(4)]
+        recip = [keep.tile([P, 2], F32, name="recip%d" % u) for u in range(UNITS)]
+        res = [keep.tile([P, 2, E], F32, name="res%d" % u) for u in range(UNITS)]
 
-        def exps(u, half):
-            if half == 0:
+        def exps(u, half, cols=slice(0, C)):
+            if u not in w_rows:
                 w_rows[u] = ring.tile([P, PACK, C], BF16, name="w_rows", tag="w_rows")
             for r in range(2):
                 nc.scalar.activation(
-                    out=w_rows[u][:, 2 * half + r, :],
-                    in_=banks[u, half][:, r, :],
+                    out=w_rows[u][:, 2 * half + r, cols],
+                    in_=banks[u, half][:, r, cols],
                     func=ACT.Exp,
                     bias=ln_t[:, 2 * half + r : 2 * half + r + 1],
                 )
@@ -156,7 +163,6 @@ def tile_rows_gate_gqa_kernel(tc, qT, kT, t, v, og, out):
             w_bf[u] = ring.tile([P, C, PACK], BF16, name="w_bf", tag="w_bf", align_bytes=64)
             w_codes[u] = ring.tile([P, C], U32, name="w_codes", tag="w_codes", align_bytes=64)
             w_scales[u] = ring.tile([P, C], U8, name="w_scales", tag="w_scales", align_bytes=64)
-            y[u] = psum.tile([P, 2, E], F32, name="y", tag="y", bufs=2)
 
         def w_interleave(u, cols=slice(0, C)):
             interleave(w_bf[u][:, cols, :], w_rows[u][:, :, cols])
@@ -165,6 +171,8 @@ def tile_rows_gate_gqa_kernel(tc, qT, kT, t, v, og, out):
             quantize(w_codes[u][:, cols], w_scales[u][:, cols], w_bf[u][:, cols, :].rearrange("p c j -> p (c j)"))
 
         def values(u, c):
+            if c == 0:
+                y[u] = psum.tile([P, 2, E], F32, name="y", tag="y", bufs=2)
             cols = slice(c * P, (c + 1) * P)
             nc.tensor.matmul_mx(
                 out=y[u][:, c, :],
@@ -176,36 +184,37 @@ def tile_rows_gate_gqa_kernel(tc, qT, kT, t, v, og, out):
                 stop=True,
             )
 
-        def tanh_pair(i):
+        def tanh(i, heads=slice(0, 2)):
             pair, ch = divmod(i, 2)
-            th[i] = ring.tile([P, 2, C], F32, name="th", tag="th")
-            nc.scalar.activation(out=th[i][:], in_=og_raw[pair][:, :, ch, :], func=ACT.Tanh, scale=0.5)
+            nc.scalar.activation(out=th[i][:, heads], in_=og_raw[pair][:, heads, ch, :], func=ACT.Tanh, scale=0.5)
 
-        def gate_pair(i):
-            gate[i] = ring.tile([P, 2, C], F32, name="gate", tag="gate")
-            if i < 3:
-                nc.vector.tensor_scalar(out=gate[i][:], in0=th[i][:], scalar1=0.5, scalar2=0.5, op0=ALU.mult, op1=ALU.add)
-            else:
-                nc.scalar.activation(out=gate[i][:], in_=th[i][:], func=ACT.Copy, scale=0.5, bias=0.5)
+        def gate_on_vector(i, heads=slice(0, 2)):
+            nc.vector.tensor_scalar(
+                out=gate[i][:, heads], in0=th[i][:, heads], scalar1=0.5, scalar2=0.5, op0=ALU.mult, op1=ALU.add
+            )
 
-        def reciprocal(u):
-            recip[u] = ring.tile([P, 2], F32, name="recip", tag="recip")
-            nc.vector.reciprocal(out=recip[u][:], in_=y[u][:, :, E - 1])
+        def reciprocal(u, cs=slice(0, 2)):
+            nc.vector.reciprocal(out=recip[u][:, cs], in_=y[u][:, cs, E - 1])
 
-        def finish(u):
+        def finish(u, c):
+            nc.vector.scalar_tensor_tensor(
+                out=res[u][:, c, :],
+                in0=y[u][:, c, :],
+                scalar=recip[u][:, c : c + 1],
+                in1=gate[u // 2][:, u % 2, c * E : (c + 1) * E],
+                op0=ALU.mult,
+                op1=ALU.mult,
+            )
+
+        def store(u):
             pair, ch, g = unit_of(u)
-            res = ring.tile([P, 2, E], F32, name="res", tag="res")
-            for c in range(2):
-                nc.vector.scalar_tensor_tensor(
-                    out=res[:, c, :],
-                    in0=y[u][:, c, :],
-                    scalar=recip[u][:, c : c + 1],
-                    in1=gate[u // 2][:, g, c * E : (c + 1) * E],
-                    op0=ALU.mult,
-                    op1=ALU.mult,
-                )
             dst = out[2 * pair + g].rearrange("(p c) e -> p c e", c=4)[:, 2 * ch : 2 * ch + 2, :]
-            nc.sync.dma_start(out=dst, in_=res[:])
+            nc.sync.dma_start(out=dst, in_=res[u][:])
+
+        def finish_unit(u):
+            finish(u, 0)
+            finish(u, 1)
+            store(u)
 
         lo, hi = slice(0, P), slice(P, C)
         top, bottom = slice(0, R), slice(R, P)
@@ -217,12 +226,9 @@ def tile_rows_gate_gqa_kernel(tc, qT, kT, t, v, og, out):
         for r in range(PACK):
             quantize(k_codes[0][:, r, 0:R], k_scales[0][:, r, 0:R], k_bf[:, r].rearrange("p s j -> p (s j)"))
         for dst, src in zip(k_window(0, top, 1), k_window(0, bottom, 0)):
-            nc.sync.dma_start(out=dst, in_=src)
+            nc.scalar.dma_start(out=dst, in_=src)
         for dst, src in zip(k_window(1, bottom, 0), k_window(0, top, 0)):
-            nc.sync.dma_start(out=dst, in_=src)
-        load_q(1)
-        load_og(0)
-        load_og(1)
+            nc.scalar.dma_start(out=dst, in_=src)
         nc.vector.scalar_tensor_tensor(out=ln_t[:], in0=ratio[:], scalar=-1.0, in1=ln0[:], op0=ALU.add, op1=ALU.add)
         inter_q(0)
         dst, src = q_views(1)
@@ -241,42 +247,53 @@ def tile_rows_gate_gqa_kernel(tc, qT, kT, t, v, og, out):
         quant_q(1)
         quantize(v_codes[:], v_scales[:], v_bf[:].rearrange("p c j -> p (c j)"))
         scores((1, 1), (2, 0))
-        inter_q(2)
 
         last = UNITS - 1
         for u in range(last):
             exps(u, 0)
             scores((u + 2, 1), (u + 3, 0))
+            if u >= 1:
+                values(u - 1, 0)
+                values(u - 1, 1)
             exps(u, 1)
-            if u in (1, 2, 4):
-                tanh_pair((1, 2, 4).index(u))
+            if u % 2 == 1:
+                tanh(u // 2)
+            if u == last - 1:
+                tanh(3, slice(0, 1))
             w_tiles(u)
             w_interleave(u)
-            if u >= 1:
-                reciprocal(u - 1)
-            if u == 2:
-                inter_q(3)
-            if u in (1, 3, 5):
-                gate_pair(u // 2)
+            if u in (0, 2):
+                inter_q(2 + u // 2)
+            if u >= 2:
+                finish_unit(u - 2)
+            if u == 1:
+                gate_on_vector(0)
             w_quant(u)
-            values(u, 0)
-            values(u, 1)
             if u in (0, 2):
                 quant_q(2 + u // 2)
             if u >= 1:
-                finish(u - 1)
-        exps(last, 0)
-        exps(last, 1)
-        tanh_pair(3)
-        gate_pair(3)
+                reciprocal(u - 1)
+            if u in (3, 5):
+                gate_on_vector(u // 2)
+        values(last - 1, 0)
+        values(last - 1, 1)
+        for cols in (lo, hi):
+            exps(last, 0, cols)
+            exps(last, 1, cols)
+        tanh(3, slice(1, 2))
+        nc.scalar.activation(out=gate[3][:, 1], in_=th[3][:, 1], func=ACT.Copy, scale=0.5, bias=0.5)
         w_tiles(last)
+        gate_on_vector(3, slice(0, 1))
+        finish_unit(last - 2)
         w_interleave(last, lo)
-        w_interleave(last, hi)
+        reciprocal(last - 1)
         w_quant(last, lo)
         values(last, 0)
+        w_interleave(last, hi)
+        finish(last - 1, 0)
         w_quant(last, hi)
         values(last, 1)
-        reciprocal(last - 1)
-        finish(last - 1)
+        finish(last - 1, 1)
+        store(last - 1)
         reciprocal(last)
-        finish(last)
+        finish_unit(last)

@@ -19,6 +19,7 @@ R = 64
 PACK = 4
 C = 256
 UNITS = 8
+SCORE_BANKS = 3
 
 
 def tile_rows_gate_gqa_kernel(tc, qT, kT, t, v, og, out):
@@ -30,34 +31,35 @@ def tile_rows_gate_gqa_kernel(tc, qT, kT, t, v, og, out):
         ctx.enter_context(tc.manual_schedule())
 
         t_raw = keep.tile([P, PACK], F32, name="t_raw")
-        k_raw = keep.tile([P, PACK, C], F32, name="k_raw")
+        k_raw = keep.tile([R, PACK, N], F32, name="k_raw")
         v_raw = keep.tile([P, PACK, E], F32, name="v_raw")
-        q_raw = [keep.tile([P, PACK, NQ], F32, name="q_raw%d" % i) for i in range(2)]
-        og_raw = [keep.tile([P, 2, 2, C], F32, name="og_raw%d" % i) for i in range(2)]
+        q_raw = [keep.tile([P, PACK, C], F32, name="q_raw%d" % i) for i in range(4)]
+        og_raw = [keep.tile([P, 2, C], F32, name="og_raw%d" % h) for h in range(H)]
 
-        def load_q(pair):
-            src = qT[2 * pair : 2 * pair + 2]
-            nc.sync.dma_start(out=q_raw[pair][:], in_=src.rearrange("h (p j) q -> (h p) j q", j=PACK))
+        def load_q(i):
+            pair, ch = divmod(i, 2)
+            src = qT[2 * pair : 2 * pair + 2, :, ch * C : (ch + 1) * C]
+            nc.sync.dma_start(out=q_raw[i][:], in_=src.rearrange("h (p j) q -> (h p) j q", j=PACK))
 
-        def load_og(pair):
-            src = og[2 * pair : 2 * pair + 2].rearrange("h (p c) e -> p h (c e)", c=4)
-            nc.sync.dma_start(out=og_raw[pair][:].rearrange("p h k x -> p h (k x)"), in_=src)
+        def by_query(rows):
+            return rows.rearrange("(k s c) e -> s k (c e)", k=2, c=2)
 
-        k_src = kT[0].rearrange("(p j) n -> p j n", j=PACK)
+        def load_og(h):
+            nc.sync.dma_start(out=og_raw[h][:], in_=by_query(og[h]))
+
         nc.sync.dma_start(out=t_raw[:], in_=t.rearrange("(p j) o -> p (j o)", j=PACK))
-        nc.sync.dma_start(out=k_raw[0:R], in_=k_src[:, :, 0:C])
-        nc.scalar.dma_start(out=k_raw[R:P], in_=k_src[:, :, C:N])
+        nc.sync.dma_start(out=k_raw[:], in_=kT[0].rearrange("(p j) n -> p j n", j=PACK))
         load_q(0)
-        nc.sync.dma_start(out=v_raw[:], in_=v[0].rearrange("(p j) e -> p j e", j=PACK))
         load_q(1)
+        nc.sync.dma_start(out=v_raw[:], in_=v[0].rearrange("(p j) e -> p j e", j=PACK))
+        load_q(2)
         load_og(0)
-        load_og(1)
 
-        k_bf = keep.tile([P, PACK, R, PACK], BF16, name="k_bf", align_bytes=64)
-        k_codes = [keep.tile([P, PACK, P], U32, name="k_codes%d" % i, align_bytes=64) for i in range(2)]
-        k_scales = [keep.tile([P, PACK, P], U8, name="k_scales%d" % i, align_bytes=64) for i in range(2)]
-        for i in range(2):
-            nc.vector.memset(k_scales[i][:].rearrange("p r s -> p (r s)").bitcast(I32), 0)
+        k_bf = [keep.tile([R, 2, P, PACK], BF16, name="k_bf%d" % i, align_bytes=64) for i in range(2)]
+        k_mx = keep.tile([P, N + N // 4], U32, name="k_mx", align_bytes=64)
+        k_codes = k_mx[:, 0:N]
+        k_scales = k_mx[:, N : N + N // 4].bitcast(U8)
+        nc.vector.memset(k_mx[0:R, N : N + N // 4].bitcast(I32), 0)
 
         t_abs = keep.tile([P, PACK], F32, name="t_abs")
         t_pos2 = keep.tile([P, PACK], F32, name="t_pos2")
@@ -78,222 +80,174 @@ def tile_rows_gate_gqa_kernel(tc, qT, kT, t, v, og, out):
         v_bf = keep.tile([P, E, PACK], BF16, name="v_bf", align_bytes=64)
         v_codes = keep.tile([P, E], U32, name="v_codes", align_bytes=64)
         v_scales = keep.tile([P, E], U8, name="v_scales", align_bytes=64)
+        th = [keep.tile([P, 2, C], F32, name="th%d" % h) for h in range(H)]
+        gate = [keep.tile([P, 2, C], F32, name="gate%d" % h) for h in range(H)]
+        recip = [keep.tile([P, 2], F32, name="recip%d" % u) for u in range(UNITS)]
+        res = [keep.tile([P, 2 * E], F32, name="res%d" % u) for u in range(UNITS)]
+        banks, w_rows, w_bf, w_codes, w_scales, y = {}, {}, {}, {}, {}, {}
 
         def quantize(codes, scales, grouped):
             nc.vector.quantize_mx(out=codes.bitcast(FP8X4), scales=scales, in_=grouped)
 
-        def interleave(dst, src):
-            nc.vector.tensor_copy(
-                out=dst.rearrange("p (c i) j -> p c j i", i=4),
-                in_=src.rearrange("p j (c i) -> p c j i", i=4),
-            )
+        def k_views(i):
+            src = k_raw[:].rearrange("p j (s r) -> p s j r", r=PACK)[:, :, :, 2 * i : 2 * i + 2]
+            return k_bf[i][:].rearrange("p r s j -> p s j r"), src
+
+        def quant_k(r):
+            toks = slice(r * P, (r + 1) * P)
+            quantize(k_codes[0:R, toks], k_scales[0:R, toks], k_bf[r // 2][:, r % 2].rearrange("p s j -> p (s j)"))
 
         def q_views(i):
-            pair, ch = divmod(i, 2)
-            src = q_raw[pair][:].rearrange("p j (s c) -> p s j c", c=4)[:, :, :, 2 * ch : 2 * ch + 2]
-            return q_bf[i][:].rearrange("p (c s) j -> p s j c", c=2), src
+            dst = q_bf[i][:].rearrange("p (c a b) j -> p a j b c", c=2, b=2)
+            return dst, q_raw[i][:].rearrange("p j (a b c) -> p a j b c", b=2, c=2)
 
         def inter_q(i):
             dst, src = q_views(i)
             nc.vector.tensor_copy(out=dst, in_=src)
 
-        def k_window(g, rows, half):
-            codes = k_codes[g][rows, :, half * R : (half + 1) * R].bitcast(I32)
-            scales = k_scales[g][rows, :, half * R : (half + 1) * R].bitcast(I32)
-            return codes, scales
+        def quant_q(i):
+            quantize(q_codes[i][:], q_scales[i][:], q_bf[i][:].rearrange("p c j -> p (c j)"))
 
-        def quant_q(i, cols=slice(0, C)):
-            quantize(q_codes[i][:, cols], q_scales[i][:, cols], q_bf[i][:, cols, :].rearrange("p c j -> p (c j)"))
-
-        banks = {}
-
-        def unit_of(u):
-            pair, rest = divmod(u, 4)
-            ch, g = divmod(rest, 2)
-            return pair, ch, g
-
-        def score_calls(u, half):
-            pair, ch, g = unit_of(u)
-            bank = psum.tile([P, 2, C], F32, name="score%d" % g, tag="score%d" % g, bufs=3)
-            banks[u, half] = bank
+        def scores(n):
+            if n >= 2 * UNITS:
+                return
+            u, half = divmod(n, 2)
+            h, ch = divmod(u, 2)
+            g, qi = h % 2, 2 * (h // 2) + ch
             rows = slice(R * g, R * g + R)
-            calls = []
-            for c in range(2):
-                for r in range(2):
-                    calls.append((bank, g, rows, half, r, 2 * pair + ch, c))
-            return calls
+            banks[n] = psum.tile([P, 2, C], F32, name="score%d" % g, tag="score%d" % g, bufs=SCORE_BANKS)
+            for r in range(2):
+                toks = slice((2 * half + r) * P, (2 * half + r + 1) * P)
+                for c in range(2):
+                    cols = slice(c * P, (c + 1) * P)
+                    nc.tensor.matmul_mx(
+                        out=banks[n][:, r, cols],
+                        lhsT=k_codes[rows, toks].bitcast(FP8X4),
+                        lhsT_scale=k_scales[rows, toks],
+                        rhs=q_codes[qi][rows, cols].bitcast(FP8X4),
+                        rhs_scale=q_scales[qi][rows, cols],
+                        start=True,
+                        stop=True,
+                    )
 
-        def score(call):
-            bank, g, rows, half, r, qi, c = call
-            cols = slice(c * P, (c + 1) * P)
-            nc.tensor.matmul_mx(
-                out=bank[:, r, cols],
-                lhsT=k_codes[g][rows, 2 * half + r, :].bitcast(FP8X4),
-                lhsT_scale=k_scales[g][rows, 2 * half + r, :],
-                rhs=q_codes[qi][rows, cols].bitcast(FP8X4),
-                rhs_scale=q_scales[qi][rows, cols],
-                start=True,
-                stop=True,
-            )
-
-        def scores(*halves):
-            lists = [score_calls(u, half) for u, half in halves if u < UNITS]
-            for group in zip(*lists):
-                for call in group:
-                    score(call)
-
-        w_rows, w_bf, w_codes, w_scales, y = {}, {}, {}, {}, {}
-        th = [keep.tile([P, 2, C], F32, name="th%d" % i) for i in range(4)]
-        gate = [keep.tile([P, 2, C], F32, name="gate%d" % i) for i in range(4)]
-        recip = [keep.tile([P, 2], F32, name="recip%d" % u) for u in range(UNITS)]
-        res = [keep.tile([P, 2, E], F32, name="res%d" % u) for u in range(UNITS)]
-
-        def exps(u, half, cols=slice(0, C)):
-            if u not in w_rows:
+        def exps(n):
+            u, half = divmod(n, 2)
+            if half == 0:
                 w_rows[u] = ring.tile([P, PACK, C], BF16, name="w_rows", tag="w_rows")
             for r in range(2):
+                place = 2 * half + r
                 nc.scalar.activation(
-                    out=w_rows[u][:, 2 * half + r, cols],
-                    in_=banks[u, half][:, r, cols],
-                    func=ACT.Exp,
-                    bias=ln_t[:, 2 * half + r : 2 * half + r + 1],
+                    out=w_rows[u][:, place, :], in_=banks[n][:, r, :], func=ACT.Exp, bias=ln_t[:, place : place + 1]
                 )
 
-        def w_tiles(u):
+        def w_interleave(u):
             w_bf[u] = ring.tile([P, C, PACK], BF16, name="w_bf", tag="w_bf", align_bytes=64)
+            nc.vector.tensor_copy(
+                out=w_bf[u][:].rearrange("p (a b) j -> p a j b", b=4),
+                in_=w_rows[u][:].rearrange("p j (a b) -> p a j b", b=4),
+            )
+
+        def w_quant(u):
             w_codes[u] = ring.tile([P, C], U32, name="w_codes", tag="w_codes", align_bytes=64)
             w_scales[u] = ring.tile([P, C], U8, name="w_scales", tag="w_scales", align_bytes=64)
+            quantize(w_codes[u][:], w_scales[u][:], w_bf[u][:].rearrange("p c j -> p (c j)"))
 
-        def w_interleave(u, cols=slice(0, C)):
-            interleave(w_bf[u][:, cols, :], w_rows[u][:, :, cols])
+        def values(u):
+            y[u] = psum.tile([P, 2, E], F32, name="y", tag="y", bufs=2)
+            for c in range(2):
+                cols = slice(c * P, (c + 1) * P)
+                nc.tensor.matmul_mx(
+                    out=y[u][:, c, :],
+                    lhsT=w_codes[u][:, cols].bitcast(FP8X4),
+                    lhsT_scale=w_scales[u][:, cols],
+                    rhs=v_codes[:].bitcast(FP8X4),
+                    rhs_scale=v_scales[:],
+                    start=True,
+                    stop=True,
+                )
 
-        def w_quant(u, cols=slice(0, C)):
-            quantize(w_codes[u][:, cols], w_scales[u][:, cols], w_bf[u][:, cols, :].rearrange("p c j -> p (c j)"))
+        def reciprocal(u):
+            nc.vector.reciprocal(out=recip[u][:], in_=y[u][:, :, E - 1])
 
-        def values(u, c):
-            if c == 0:
-                y[u] = psum.tile([P, 2, E], F32, name="y", tag="y", bufs=2)
-            cols = slice(c * P, (c + 1) * P)
-            nc.tensor.matmul_mx(
-                out=y[u][:, c, :],
-                lhsT=w_codes[u][:, cols].bitcast(FP8X4),
-                lhsT_scale=w_scales[u][:, cols],
-                rhs=v_codes[:].bitcast(FP8X4),
-                rhs_scale=v_scales[:],
-                start=True,
-                stop=True,
-            )
+        def finish(u):
+            h, ch = divmod(u, 2)
+            for c in range(2):
+                cols = slice(c * E, (c + 1) * E)
+                nc.vector.scalar_tensor_tensor(
+                    out=res[u][:, cols],
+                    in0=y[u][:, c, :],
+                    scalar=recip[u][:, c : c + 1],
+                    in1=gate[h][:, ch, cols],
+                    op0=ALU.mult,
+                    op1=ALU.mult,
+                )
+            nc.sync.dma_start(out=by_query(out[h])[:, ch, :], in_=res[u][:])
 
-        def tanh(i, heads=slice(0, 2)):
-            pair, ch = divmod(i, 2)
-            nc.scalar.activation(out=th[i][:, heads], in_=og_raw[pair][:, heads, ch, :], func=ACT.Tanh, scale=0.5)
-
-        def gate_on_vector(i, heads=slice(0, 2)):
-            nc.vector.tensor_scalar(
-                out=gate[i][:, heads], in0=th[i][:, heads], scalar1=0.5, scalar2=0.5, op0=ALU.mult, op1=ALU.add
-            )
-
-        def reciprocal(u, cs=slice(0, 2)):
-            nc.vector.reciprocal(out=recip[u][:, cs], in_=y[u][:, cs, E - 1])
-
-        def finish(u, c):
-            nc.vector.scalar_tensor_tensor(
-                out=res[u][:, c, :],
-                in0=y[u][:, c, :],
-                scalar=recip[u][:, c : c + 1],
-                in1=gate[u // 2][:, u % 2, c * E : (c + 1) * E],
-                op0=ALU.mult,
-                op1=ALU.mult,
-            )
-
-        def store(u):
-            pair, ch, g = unit_of(u)
-            dst = out[2 * pair + g].rearrange("(p c) e -> p c e", c=4)[:, 2 * ch : 2 * ch + 2, :]
-            nc.sync.dma_start(out=dst, in_=res[u][:])
-
-        def finish_unit(u):
-            finish(u, 0)
-            finish(u, 1)
-            store(u)
-
-        lo, hi = slice(0, P), slice(P, C)
-        top, bottom = slice(0, R), slice(R, P)
-        nc.vector.tensor_copy(
-            out=k_bf[:].rearrange("p r s j -> p s j r"),
-            in_=k_raw[:].rearrange("p j (s r) -> p s j r", r=PACK),
-        )
-        nc.vector.tensor_tensor(out=ratio[:], in0=inv0[:], in1=t_abs[:], op=ALU.mult)
-        for r in range(PACK):
-            quantize(k_codes[0][:, r, 0:R], k_scales[0][:, r, 0:R], k_bf[:, r].rearrange("p s j -> p (s j)"))
-        for dst, src in zip(k_window(0, top, 1), k_window(0, bottom, 0)):
-            nc.scalar.dma_start(out=dst, in_=src)
-        for dst, src in zip(k_window(1, bottom, 0), k_window(0, top, 0)):
-            nc.scalar.dma_start(out=dst, in_=src)
-        nc.vector.scalar_tensor_tensor(out=ln_t[:], in0=ratio[:], scalar=-1.0, in1=ln0[:], op0=ALU.add, op1=ALU.add)
-        inter_q(0)
-        dst, src = q_views(1)
+        dst, src = k_views(0)
+        nc.vector.tensor_copy(out=dst, in_=src)
+        dst, src = k_views(1)
         nc.scalar.copy(out=dst, in_=src)
-        for dst, src in zip(k_window(1, bottom, 1), k_window(0, bottom, 0)):
-            nc.vector.tensor_copy(out=dst, in_=src)
+        quant_k(0)
+        quant_k(1)
+        inter_q(0)
+        nc.vector.tensor_tensor(out=ratio[:], in0=inv0[:], in1=t_abs[:], op=ALU.mult)
         quant_q(0)
-        scores((0, 0))
-        scores((0, 1), (1, 0))
+        nc.vector.scalar_tensor_tensor(out=ln_t[:], in0=ratio[:], scalar=-1.0, in1=ln0[:], op0=ALU.add, op1=ALU.add)
+        scores(0)
+        quant_k(2)
+        quant_k(3)
+        scores(1)
+        nc.sync.dma_start(out=k_mx[R:P, :].bitcast(I32), in_=k_mx[0:R, :].bitcast(I32))
+        load_q(3)
+        for h in range(1, H):
+            load_og(h)
+        inter_q(1)
         nc.vector.tensor_tensor(
-            out=v_bf[:].rearrange("p (c i) j -> p c j i", i=4),
-            in0=v_raw[:].rearrange("p j (c i) -> p c j i", i=4),
+            out=v_bf[:].rearrange("p (a b) j -> p a j b", b=4),
+            in0=v_raw[:].rearrange("p j (a b) -> p a j b", b=4),
             in1=t_sign[:].unsqueeze(1).unsqueeze(3).to_broadcast([P, E // 4, PACK, 4]),
             op=ALU.mult,
         )
         quant_q(1)
         quantize(v_codes[:], v_scales[:], v_bf[:].rearrange("p c j -> p (c j)"))
-        scores((1, 1), (2, 0))
+        scores(2)
 
         last = UNITS - 1
         for u in range(last):
-            exps(u, 0)
-            scores((u + 2, 1), (u + 3, 0))
+            h, ch = divmod(u, 2)
+            exps(2 * u)
+            scores(2 * u + SCORE_BANKS)
             if u >= 1:
-                values(u - 1, 0)
-                values(u - 1, 1)
-            exps(u, 1)
-            if u % 2 == 1:
-                tanh(u // 2)
-            if u == last - 1:
-                tanh(3, slice(0, 1))
-            w_tiles(u)
+                values(u - 1)
+            exps(2 * u + 1)
+            scores(2 * u + 1 + SCORE_BANKS)
+            if ch == 1:
+                nc.scalar.activation(out=th[h][:], in_=og_raw[h][:], func=ACT.Tanh, scale=0.5)
             w_interleave(u)
-            if u in (0, 2):
-                inter_q(2 + u // 2)
+            if u < 2:
+                inter_q(2 + u)
+            if ch == 1:
+                nc.vector.tensor_scalar(
+                    out=gate[h][:], in0=th[h][:], scalar1=0.5, scalar2=0.5, op0=ALU.mult, op1=ALU.add
+                )
             if u >= 2:
-                finish_unit(u - 2)
-            if u == 1:
-                gate_on_vector(0)
+                finish(u - 2)
             w_quant(u)
-            if u in (0, 2):
-                quant_q(2 + u // 2)
+            if u < 2:
+                quant_q(2 + u)
             if u >= 1:
                 reciprocal(u - 1)
-            if u in (3, 5):
-                gate_on_vector(u // 2)
-        values(last - 1, 0)
-        values(last - 1, 1)
-        for cols in (lo, hi):
-            exps(last, 0, cols)
-            exps(last, 1, cols)
-        tanh(3, slice(1, 2))
-        nc.scalar.activation(out=gate[3][:, 1], in_=th[3][:, 1], func=ACT.Copy, scale=0.5, bias=0.5)
-        w_tiles(last)
-        gate_on_vector(3, slice(0, 1))
-        finish_unit(last - 2)
-        w_interleave(last, lo)
+        exps(2 * last)
+        values(last - 1)
+        exps(2 * last + 1)
+        for ch in range(2):
+            nc.scalar.activation(out=th[H - 1][:, ch], in_=og_raw[H - 1][:, ch], func=ACT.Tanh, scale=0.5)
+            nc.scalar.activation(out=gate[H - 1][:, ch], in_=th[H - 1][:, ch], func=ACT.Copy, scale=0.5, bias=0.5)
+        finish(last - 2)
+        w_interleave(last)
         reciprocal(last - 1)
-        w_quant(last, lo)
-        values(last, 0)
-        w_interleave(last, hi)
-        finish(last - 1, 0)
-        w_quant(last, hi)
-        values(last, 1)
-        finish(last - 1, 1)
-        store(last - 1)
+        w_quant(last)
+        values(last)
+        finish(last - 1)
         reciprocal(last)
-        finish_unit(last)
+        finish(last)

@@ -20,46 +20,43 @@ PACK = 4
 C = 256
 UNITS = 8
 SCORE_BANKS = 3
+W_BUFS = 3
 
 
 def tile_rows_gate_gqa_kernel(tc, qT, kT, t, v, og, out):
     nc = tc.nc
     with ExitStack() as ctx:
         keep = ctx.enter_context(tc.tile_pool(name="keep", bufs=1))
-        ring = ctx.enter_context(tc.tile_pool(name="ring", bufs=3))
+        ring = ctx.enter_context(tc.tile_pool(name="ring", bufs=W_BUFS))
         psum = ctx.enter_context(tc.psum_pool(name="psum", bufs=1))
         ctx.enter_context(tc.manual_schedule())
 
         t_raw = keep.tile([P, PACK], F32, name="t_raw")
-        k_raw = keep.tile([R, PACK, N], F32, name="k_raw")
+        k_raw = keep.tile([P, PACK, C], F32, name="k_raw")
         v_raw = keep.tile([P, PACK, E], F32, name="v_raw")
-        q_raw = [keep.tile([P, PACK, C], F32, name="q_raw%d" % i) for i in range(4)]
-        og_raw = [keep.tile([P, 2, C], F32, name="og_raw%d" % h) for h in range(H)]
+        q_raw = [keep.tile([P, PACK, NQ], F32, name="q_raw%d" % pair) for pair in range(2)]
+        og_first = [keep.tile([P, 2, C], F32, name="og_first%d" % h) for h in range(2)]
+        og_last = keep.tile([P, 2, 2, C], F32, name="og_last")
 
-        def load_q(i):
-            pair, ch = divmod(i, 2)
-            src = qT[2 * pair : 2 * pair + 2, :, ch * C : (ch + 1) * C]
-            nc.sync.dma_start(out=q_raw[i][:], in_=src.rearrange("h (p j) q -> (h p) j q", j=PACK))
+        def load_q(pair):
+            src = qT[2 * pair : 2 * pair + 2].rearrange("h (p j) q -> (h p) j q", j=PACK)
+            nc.sync.dma_start(out=q_raw[pair][:], in_=src)
 
         def by_query(rows):
-            return rows.rearrange("(k s c) e -> s k (c e)", k=2, c=2)
-
-        def load_og(h):
-            nc.sync.dma_start(out=og_raw[h][:], in_=by_query(og[h]))
+            return rows.rearrange("(s k c) e -> s k (c e)", k=2, c=2)
 
         nc.sync.dma_start(out=t_raw[:], in_=t.rearrange("(p j) o -> p (j o)", j=PACK))
-        nc.sync.dma_start(out=k_raw[:], in_=kT[0].rearrange("(p j) n -> p j n", j=PACK))
+        k_src = kT[0].rearrange("(p j) n -> p j n", j=PACK)
+        nc.sync.dma_start(out=k_raw[0:R], in_=k_src[:, :, 0:C])
+        nc.scalar.dma_start(out=k_raw[R:P], in_=k_src[:, :, C:N])
         load_q(0)
-        load_q(1)
-        nc.sync.dma_start(out=v_raw[:], in_=v[0].rearrange("(p j) e -> p j e", j=PACK))
-        load_q(2)
-        load_og(0)
+        nc.sync.dma_start(out=og_first[0][:], in_=by_query(og[0]))
 
-        k_bf = [keep.tile([R, 2, P, PACK], BF16, name="k_bf%d" % i, align_bytes=64) for i in range(2)]
-        k_mx = keep.tile([P, N + N // 4], U32, name="k_mx", align_bytes=64)
-        k_codes = k_mx[:, 0:N]
-        k_scales = k_mx[:, N : N + N // 4].bitcast(U8)
-        nc.vector.memset(k_mx[0:R, N : N + N // 4].bitcast(I32), 0)
+        k_bf = keep.tile([P, PACK, R, PACK], BF16, name="k_bf", align_bytes=64)
+        k_codes = [keep.tile([P, PACK, P], U32, name="k_codes%d" % g, align_bytes=64) for g in range(2)]
+        k_scales = [keep.tile([P, PACK, P], U8, name="k_scales%d" % g, align_bytes=64) for g in range(2)]
+        for g in range(2):
+            nc.vector.memset(k_scales[g][:].rearrange("p r s -> p (r s)").bitcast(I32), 0)
 
         t_abs = keep.tile([P, PACK], F32, name="t_abs")
         t_pos2 = keep.tile([P, PACK], F32, name="t_pos2")
@@ -80,8 +77,9 @@ def tile_rows_gate_gqa_kernel(tc, qT, kT, t, v, og, out):
         v_bf = keep.tile([P, E, PACK], BF16, name="v_bf", align_bytes=64)
         v_codes = keep.tile([P, E], U32, name="v_codes", align_bytes=64)
         v_scales = keep.tile([P, E], U8, name="v_scales", align_bytes=64)
-        th = [keep.tile([P, 2, C], F32, name="th%d" % h) for h in range(H)]
-        gate = [keep.tile([P, 2, C], F32, name="gate%d" % h) for h in range(H)]
+        og_piece = [og_first[0][:], og_first[1][:], og_last[:, :, 0, :], og_last[:, :, 1, :]]
+        th = [keep.tile([P, 2, C], F32, name="th%d" % i) for i in range(4)]
+        gate = [keep.tile([P, 2, C], F32, name="gate%d" % i) for i in range(4)]
         recip = [keep.tile([P, 2], F32, name="recip%d" % u) for u in range(UNITS)]
         res = [keep.tile([P, 2 * E], F32, name="res%d" % u) for u in range(UNITS)]
         banks, w_rows, w_bf, w_codes, w_scales, y = {}, {}, {}, {}, {}, {}
@@ -89,68 +87,65 @@ def tile_rows_gate_gqa_kernel(tc, qT, kT, t, v, og, out):
         def quantize(codes, scales, grouped):
             nc.vector.quantize_mx(out=codes.bitcast(FP8X4), scales=scales, in_=grouped)
 
-        def k_views(i):
-            src = k_raw[:].rearrange("p j (s r) -> p s j r", r=PACK)[:, :, :, 2 * i : 2 * i + 2]
-            return k_bf[i][:].rearrange("p r s j -> p s j r"), src
-
-        def quant_k(r):
-            toks = slice(r * P, (r + 1) * P)
-            quantize(k_codes[0:R, toks], k_scales[0:R, toks], k_bf[r // 2][:, r % 2].rearrange("p s j -> p (s j)"))
+        def k_window(g, rows, half):
+            codes = k_codes[g][rows, :, half * R : (half + 1) * R].bitcast(I32)
+            scales = k_scales[g][rows, :, half * R : (half + 1) * R].bitcast(I32)
+            return codes, scales
 
         def q_views(i):
-            dst = q_bf[i][:].rearrange("p (c a b) j -> p a j b c", c=2, b=2)
-            return dst, q_raw[i][:].rearrange("p j (a b c) -> p a j b c", b=2, c=2)
+            pair, ch = divmod(i, 2)
+            src = q_raw[pair][:].rearrange("p j (s c) -> p s j c", c=4)[:, :, :, 2 * ch : 2 * ch + 2]
+            return q_bf[i][:].rearrange("p (c s) j -> p s j c", c=2), src
 
-        def inter_q(i):
+        def interleave_q(i):
             dst, src = q_views(i)
             nc.vector.tensor_copy(out=dst, in_=src)
 
-        def quant_q(i):
+        def quantize_q(i):
             quantize(q_codes[i][:], q_scales[i][:], q_bf[i][:].rearrange("p c j -> p (c j)"))
 
-        def scores(n):
-            if n >= 2 * UNITS:
-                return
-            u, half = divmod(n, 2)
-            h, ch = divmod(u, 2)
-            g, qi = h % 2, 2 * (h // 2) + ch
-            rows = slice(R * g, R * g + R)
-            banks[n] = psum.tile([P, 2, C], F32, name="score%d" % g, tag="score%d" % g, bufs=SCORE_BANKS)
-            for r in range(2):
-                toks = slice((2 * half + r) * P, (2 * half + r + 1) * P)
-                for c in range(2):
+        def score_calls(u, half):
+            g = u % 2
+            bank = psum.tile([P, 2, C], F32, name="score%d" % g, tag="score%d" % g, bufs=SCORE_BANKS)
+            banks[u, half] = bank
+            return [(bank, u, half, rr, c) for rr in range(2) for c in range(2)]
+
+        def scores(half, *units):
+            for group in zip(*[score_calls(u, half) for u in units]):
+                for bank, u, half, rr, c in group:
+                    g, i = u % 2, u // 2
+                    rows = slice(R * g, R * g + R)
                     cols = slice(c * P, (c + 1) * P)
                     nc.tensor.matmul_mx(
-                        out=banks[n][:, r, cols],
-                        lhsT=k_codes[rows, toks].bitcast(FP8X4),
-                        lhsT_scale=k_scales[rows, toks],
-                        rhs=q_codes[qi][rows, cols].bitcast(FP8X4),
-                        rhs_scale=q_scales[qi][rows, cols],
+                        out=bank[:, rr, cols],
+                        lhsT=k_codes[g][rows, 2 * half + rr, :].bitcast(FP8X4),
+                        lhsT_scale=k_scales[g][rows, 2 * half + rr, :],
+                        rhs=q_codes[i][rows, cols].bitcast(FP8X4),
+                        rhs_scale=q_scales[i][rows, cols],
                         start=True,
                         stop=True,
                     )
 
-        def exps(n):
-            u, half = divmod(n, 2)
+        def exps(u, half):
             if half == 0:
                 w_rows[u] = ring.tile([P, PACK, C], BF16, name="w_rows", tag="w_rows")
-            for r in range(2):
-                place = 2 * half + r
+            for rr in range(2):
+                r = 2 * half + rr
                 nc.scalar.activation(
-                    out=w_rows[u][:, place, :], in_=banks[n][:, r, :], func=ACT.Exp, bias=ln_t[:, place : place + 1]
+                    out=w_rows[u][:, r, :], in_=banks[u, half][:, rr, :], func=ACT.Exp, bias=ln_t[:, r : r + 1]
                 )
 
-        def w_interleave(u):
+        def interleave_w(u):
             w_bf[u] = ring.tile([P, C, PACK], BF16, name="w_bf", tag="w_bf", align_bytes=64)
             nc.vector.tensor_copy(
-                out=w_bf[u][:].rearrange("p (a b) j -> p a j b", b=4),
-                in_=w_rows[u][:].rearrange("p j (a b) -> p a j b", b=4),
+                out=w_bf[u][:].rearrange("p (a b) r -> p a r b", b=4),
+                in_=w_rows[u][:].rearrange("p r (a b) -> p a r b", b=4),
             )
 
-        def w_quant(u):
+        def quantize_w(u):
             w_codes[u] = ring.tile([P, C], U32, name="w_codes", tag="w_codes", align_bytes=64)
             w_scales[u] = ring.tile([P, C], U8, name="w_scales", tag="w_scales", align_bytes=64)
-            quantize(w_codes[u][:], w_scales[u][:], w_bf[u][:].rearrange("p c j -> p (c j)"))
+            quantize(w_codes[u][:], w_scales[u][:], w_bf[u][:].rearrange("p q r -> p (q r)"))
 
         def values(u):
             y[u] = psum.tile([P, 2, E], F32, name="y", tag="y", bufs=2)
@@ -169,84 +164,96 @@ def tile_rows_gate_gqa_kernel(tc, qT, kT, t, v, og, out):
         def reciprocal(u):
             nc.vector.reciprocal(out=recip[u][:], in_=y[u][:, :, E - 1])
 
+        def tanh(i):
+            nc.scalar.activation(out=th[i][:], in_=og_piece[i], func=ACT.Tanh, scale=0.5)
+
+        def gate_on_vector(i):
+            nc.vector.tensor_scalar(out=gate[i][:], in0=th[i][:], scalar1=0.5, scalar2=0.5, op0=ALU.mult, op1=ALU.add)
+
         def finish(u):
-            h, ch = divmod(u, 2)
+            pair, ch, g = u // 4, (u // 2) % 2, u % 2
+            gate_u = gate[g][:, ch] if pair == 0 else gate[2 + ch][:, g]
             for c in range(2):
                 cols = slice(c * E, (c + 1) * E)
                 nc.vector.scalar_tensor_tensor(
                     out=res[u][:, cols],
                     in0=y[u][:, c, :],
                     scalar=recip[u][:, c : c + 1],
-                    in1=gate[h][:, ch, cols],
+                    in1=gate_u[:, cols],
                     op0=ALU.mult,
                     op1=ALU.mult,
                 )
-            nc.sync.dma_start(out=by_query(out[h])[:, ch, :], in_=res[u][:])
+            nc.sync.dma_start(out=by_query(out[2 * pair + g])[:, ch, :], in_=res[u][:])
 
-        dst, src = k_views(0)
-        nc.vector.tensor_copy(out=dst, in_=src)
-        dst, src = k_views(1)
-        nc.scalar.copy(out=dst, in_=src)
-        quant_k(0)
-        quant_k(1)
-        inter_q(0)
+        nc.vector.tensor_copy(
+            out=k_bf[:].rearrange("p r s j -> p s j r"),
+            in_=k_raw[:].rearrange("p j (s r) -> p s j r", r=PACK),
+        )
+        for r in range(PACK):
+            quantize(k_codes[0][:, r, 0:R], k_scales[0][:, r, 0:R], k_bf[:, r].rearrange("p s j -> p (s j)"))
+        top, bottom = slice(0, R), slice(R, P)
+        for dst, src in zip(k_window(0, top, 1), k_window(0, bottom, 0)):
+            nc.sync.dma_start(out=dst, in_=src)
+        for dst, src in zip(k_window(1, bottom, 0), k_window(0, top, 0)):
+            nc.sync.dma_start(out=dst, in_=src)
+        nc.sync.dma_start(out=v_raw[:], in_=v[0].rearrange("(p r) e -> p r e", r=PACK))
+        load_q(1)
+        nc.sync.dma_start(out=og_first[1][:], in_=by_query(og[1]))
+        nc.sync.dma_start(
+            out=og_last[:].rearrange("p h k x -> p h (k x)"), in_=og[2:4].rearrange("h (s c) e -> s h (c e)", c=4)
+        )
         nc.vector.tensor_tensor(out=ratio[:], in0=inv0[:], in1=t_abs[:], op=ALU.mult)
-        quant_q(0)
+        for dst, src in zip(k_window(1, bottom, 1), k_window(0, bottom, 0)):
+            nc.vector.tensor_copy(out=dst, in_=src)
+        interleave_q(0)
+        dst, src = q_views(1)
+        nc.scalar.copy(out=dst, in_=src)
         nc.vector.scalar_tensor_tensor(out=ln_t[:], in0=ratio[:], scalar=-1.0, in1=ln0[:], op0=ALU.add, op1=ALU.add)
-        scores(0)
-        quant_k(2)
-        quant_k(3)
-        scores(1)
-        nc.sync.dma_start(out=k_mx[R:P, :].bitcast(I32), in_=k_mx[0:R, :].bitcast(I32))
-        load_q(3)
-        for h in range(1, H):
-            load_og(h)
-        inter_q(1)
+        quantize_q(0)
+        for u in range(2):
+            scores(0, u)
+            scores(1, u)
+        tanh(0)
+        quantize_q(1)
         nc.vector.tensor_tensor(
-            out=v_bf[:].rearrange("p (a b) j -> p a j b", b=4),
-            in0=v_raw[:].rearrange("p j (a b) -> p a j b", b=4),
+            out=v_bf[:].rearrange("p (a b) r -> p a r b", b=4),
+            in0=v_raw[:].rearrange("p r (a b) -> p a r b", b=4),
             in1=t_sign[:].unsqueeze(1).unsqueeze(3).to_broadcast([P, E // 4, PACK, 4]),
             op=ALU.mult,
         )
-        quant_q(1)
-        quantize(v_codes[:], v_scales[:], v_bf[:].rearrange("p c j -> p (c j)"))
-        scores(2)
+        gate_on_vector(0)
+        quantize(v_codes[:], v_scales[:], v_bf[:].rearrange("p e r -> p (e r)"))
 
         last = UNITS - 1
-        for u in range(last):
-            h, ch = divmod(u, 2)
-            exps(2 * u)
-            scores(2 * u + SCORE_BANKS)
+        gate_piece_at = {2: 1, 5: 2}
+        for u in range(UNITS):
+            exps(u, 0)
+            ahead = 2 * (u // 2 + 1)
+            if ahead < UNITS:
+                scores(u % 2, ahead, ahead + 1)
             if u >= 1:
                 values(u - 1)
-            exps(2 * u + 1)
-            scores(2 * u + 1 + SCORE_BANKS)
-            if ch == 1:
-                nc.scalar.activation(out=th[h][:], in_=og_raw[h][:], func=ACT.Tanh, scale=0.5)
-            w_interleave(u)
+            exps(u, 1)
+            if u in gate_piece_at:
+                tanh(gate_piece_at[u])
+            if u == last:
+                for g in range(2):
+                    nc.scalar.activation(out=th[3][:, g], in_=og_piece[3][:, g], func=ACT.Tanh, scale=0.5)
+                    nc.scalar.activation(out=gate[3][:, g], in_=th[3][:, g], func=ACT.Copy, scale=0.5, bias=0.5)
+            interleave_w(u)
             if u < 2:
-                inter_q(2 + u)
-            if ch == 1:
-                nc.vector.tensor_scalar(
-                    out=gate[h][:], in0=th[h][:], scalar1=0.5, scalar2=0.5, op0=ALU.mult, op1=ALU.add
-                )
+                interleave_q(2 + u)
             if u >= 2:
                 finish(u - 2)
-            w_quant(u)
-            if u < 2:
-                quant_q(2 + u)
-            if u >= 1:
+            if u == last:
                 reciprocal(u - 1)
-        exps(2 * last)
-        values(last - 1)
-        exps(2 * last + 1)
-        for ch in range(2):
-            nc.scalar.activation(out=th[H - 1][:, ch], in_=og_raw[H - 1][:, ch], func=ACT.Tanh, scale=0.5)
-            nc.scalar.activation(out=gate[H - 1][:, ch], in_=th[H - 1][:, ch], func=ACT.Copy, scale=0.5, bias=0.5)
-        finish(last - 2)
-        w_interleave(last)
-        reciprocal(last - 1)
-        w_quant(last)
+            quantize_w(u)
+            if u < 2:
+                quantize_q(2 + u)
+            if 1 <= u < last:
+                reciprocal(u - 1)
+            if u in gate_piece_at:
+                gate_on_vector(gate_piece_at[u])
         values(last)
         finish(last - 1)
         reciprocal(last)

from contextlib import ExitStack

import concourse.mybir as mybir

H, D, NQ, N, E = 4, 256, 512, 512, 128
FLOPS = 2 * H * NQ * N * D + 2 * H * NQ * N * E

F32 = mybir.dt.float32
BF16 = mybir.dt.bfloat16
U32 = mybir.dt.uint32
U8 = mybir.dt.uint8
I32 = mybir.dt.int32
FP8X4 = mybir.dt.float8_e4m3fn_x4
ACT = mybir.ActivationFunctionType
ALU = mybir.AluOpType

P = 128
R = 64
PACK = 4
C = 256
UNITS = 8
SCORE_BANKS = 3
W_BUFS = 3


def tile_rows_gate_gqa_kernel(tc, qT, kT, t, v, og, out):
    nc = tc.nc
    with ExitStack() as ctx:
        keep = ctx.enter_context(tc.tile_pool(name="keep", bufs=1))
        ring = ctx.enter_context(tc.tile_pool(name="ring", bufs=W_BUFS))
        psum = ctx.enter_context(tc.psum_pool(name="psum", bufs=1))
        ctx.enter_context(tc.manual_schedule())

        t_raw = keep.tile([P, PACK], F32, name="t_raw")
        k_raw = keep.tile([P, PACK, C], F32, name="k_raw")
        v_raw = keep.tile([P, PACK, E], F32, name="v_raw")
        q_raw = [keep.tile([P, PACK, NQ], F32, name="q_raw%d" % pair) for pair in range(2)]
        og_first = [keep.tile([P, 2, C], F32, name="og_first%d" % h) for h in range(2)]
        og_last = keep.tile([P, 2, 2, C], F32, name="og_last")

        def load_q(pair):
            src = qT[2 * pair : 2 * pair + 2].rearrange("h (p j) q -> (h p) j q", j=PACK)
            nc.sync.dma_start(out=q_raw[pair][:], in_=src)

        def by_query(rows):
            return rows.rearrange("(s k c) e -> s k (c e)", k=2, c=2)

        nc.sync.dma_start(out=t_raw[:], in_=t.rearrange("(p j) o -> p (j o)", j=PACK))
        k_src = kT[0].rearrange("(p j) n -> p j n", j=PACK)
        nc.sync.dma_start(out=k_raw[0:R], in_=k_src[:, :, 0:C])
        nc.scalar.dma_start(out=k_raw[R:P], in_=k_src[:, :, C:N])
        load_q(0)
        nc.sync.dma_start(out=og_first[0][:], in_=by_query(og[0]))

        k_bf = keep.tile([P, PACK, R, PACK], BF16, name="k_bf", align_bytes=64)
        k_codes = [keep.tile([P, PACK, P], U32, name="k_codes%d" % g, align_bytes=64) for g in range(2)]
        k_scales = [keep.tile([P, PACK, P], U8, name="k_scales%d" % g, align_bytes=64) for g in range(2)]
        for g in range(2):
            nc.vector.memset(k_scales[g][:].rearrange("p r s -> p (r s)").bitcast(I32), 0)

        t_abs = keep.tile([P, PACK], F32, name="t_abs")
        t_pos2 = keep.tile([P, PACK], F32, name="t_pos2")
        t_sign = keep.tile([P, PACK], F32, name="t_sign")
        ln0 = keep.tile([P, PACK], F32, name="ln0")
        inv0 = keep.tile([P, PACK], F32, name="inv0")
        ratio = keep.tile([P, PACK], F32, name="ratio")
        ln_t = keep.tile([P, PACK], F32, name="ln_t")
        nc.vector.scalar_tensor_tensor(out=t_abs[:], in0=t_raw[:], scalar=-1.0, in1=t_raw[:], op0=ALU.mult, op1=ALU.max)
        nc.vector.tensor_scalar(out=t_pos2[:], in0=t_raw[:], scalar1=0.0, scalar2=2.0, op0=ALU.is_ge, op1=ALU.mult)
        nc.scalar.activation(out=ln0[:], in_=t_abs[:], func=ACT.Ln)
        nc.vector.tensor_scalar(out=t_sign[:], in0=t_pos2[:], scalar1=-1.0, scalar2=None, op0=ALU.add)
        nc.scalar.activation(out=inv0[:], in_=ln0[:], func=ACT.Exp, scale=-1.0)

        q_bf = [keep.tile([P, C, PACK], BF16, name="q_bf%d" % i, align_bytes=64) for i in range(4)]
        q_codes = [keep.tile([P, C], U32, name="q_codes%d" % i, align_bytes=64) for i in range(4)]
        q_scales = [keep.tile([P, C], U8, name="q_scales%d" % i, align_bytes=64) for i in range(4)]
        v_bf = keep.tile([P, E, PACK], BF16, name="v_bf", align_bytes=64)
        v_codes = keep.tile([P, E], U32, name="v_codes", align_bytes=64)
        v_scales = keep.tile([P, E], U8, name="v_scales", align_bytes=64)
        og_piece = [og_first[0][:], og_first[1][:], og_last[:, :, 0, :], og_last[:, :, 1, :]]
        th = [keep.tile([P, 2, C], F32, name="th%d" % i) for i in range(4)]
        gate = [keep.tile([P, 2, C], F32, name="gate%d" % i) for i in range(4)]
        recip = [keep.tile([P, 2], F32, name="recip%d" % u) for u in range(UNITS)]
        res = [keep.tile([P, 2 * E], F32, name="res%d" % u) for u in range(UNITS)]
        banks, w_rows, w_bf, w_codes, w_scales, y = {}, {}, {}, {}, {}, {}

        def quantize(codes, scales, grouped):
            nc.vector.quantize_mx(out=codes.bitcast(FP8X4), scales=scales, in_=grouped)

        def k_window(g, rows, half):
            codes = k_codes[g][rows, :, half * R : (half + 1) * R].bitcast(I32)
            scales = k_scales[g][rows, :, half * R : (half + 1) * R].bitcast(I32)
            return codes, scales

        def q_views(i):
            pair, ch = divmod(i, 2)
            src = q_raw[pair][:].rearrange("p j (s c) -> p s j c", c=4)[:, :, :, 2 * ch : 2 * ch + 2]
            return q_bf[i][:].rearrange("p (c s) j -> p s j c", c=2), src

        def interleave_q(i):
            dst, src = q_views(i)
            nc.vector.tensor_copy(out=dst, in_=src)

        def quantize_q(i):
            quantize(q_codes[i][:], q_scales[i][:], q_bf[i][:].rearrange("p c j -> p (c j)"))

        def score_calls(u, half):
            g = u % 2
            bank = psum.tile([P, 2, C], F32, name="score%d" % g, tag="score%d" % g, bufs=SCORE_BANKS)
            banks[u, half] = bank
            return [(bank, u, half, rr, c) for rr in range(2) for c in range(2)]

        def scores(half, *units):
            for group in zip(*[score_calls(u, half) for u in units]):
                for bank, u, half, rr, c in group:
                    g, i = u % 2, u // 2
                    rows = slice(R * g, R * g + R)
                    cols = slice(c * P, (c + 1) * P)
                    nc.tensor.matmul_mx(
                        out=bank[:, rr, cols],
                        lhsT=k_codes[g][rows, 2 * half + rr, :].bitcast(FP8X4),
                        lhsT_scale=k_scales[g][rows, 2 * half + rr, :],
                        rhs=q_codes[i][rows, cols].bitcast(FP8X4),
                        rhs_scale=q_scales[i][rows, cols],
                        start=True,
                        stop=True,
                    )

        def exps(u, half):
            if half == 0:
                w_rows[u] = ring.tile([P, PACK, C], BF16, name="w_rows", tag="w_rows")
            for rr in range(2):
                r = 2 * half + rr
                nc.scalar.activation(
                    out=w_rows[u][:, r, :], in_=banks[u, half][:, rr, :], func=ACT.Exp, bias=ln_t[:, r : r + 1]
                )

        def interleave_w(u):
            w_bf[u] = ring.tile([P, C, PACK], BF16, name="w_bf", tag="w_bf", align_bytes=64)
            nc.vector.tensor_copy(
                out=w_bf[u][:].rearrange("p (a b) r -> p a r b", b=4),
                in_=w_rows[u][:].rearrange("p r (a b) -> p a r b", b=4),
            )

        def quantize_w(u):
            w_codes[u] = ring.tile([P, C], U32, name="w_codes", tag="w_codes", align_bytes=64)
            w_scales[u] = ring.tile([P, C], U8, name="w_scales", tag="w_scales", align_bytes=64)
            quantize(w_codes[u][:], w_scales[u][:], w_bf[u][:].rearrange("p q r -> p (q r)"))

        def values(u):
            y[u] = psum.tile([P, 2, E], F32, name="y", tag="y", bufs=2)
            for c in range(2):
                cols = slice(c * P, (c + 1) * P)
                nc.tensor.matmul_mx(
                    out=y[u][:, c, :],
                    lhsT=w_codes[u][:, cols].bitcast(FP8X4),
                    lhsT_scale=w_scales[u][:, cols],
                    rhs=v_codes[:].bitcast(FP8X4),
                    rhs_scale=v_scales[:],
                    start=True,
                    stop=True,
                )

        def reciprocal(u):
            nc.vector.reciprocal(out=recip[u][:], in_=y[u][:, :, E - 1])

        def tanh(i):
            nc.scalar.activation(out=th[i][:], in_=og_piece[i], func=ACT.Tanh, scale=0.5)

        def gate_on_vector(i):
            nc.vector.tensor_scalar(out=gate[i][:], in0=th[i][:], scalar1=0.5, scalar2=0.5, op0=ALU.mult, op1=ALU.add)

        def finish(u):
            pair, ch, g = u // 4, (u // 2) % 2, u % 2
            gate_u = gate[g][:, ch] if pair == 0 else gate[2 + ch][:, g]
            for c in range(2):
                cols = slice(c * E, (c + 1) * E)
                nc.vector.scalar_tensor_tensor(
                    out=res[u][:, cols],
                    in0=y[u][:, c, :],
                    scalar=recip[u][:, c : c + 1],
                    in1=gate_u[:, cols],
                    op0=ALU.mult,
                    op1=ALU.mult,
                )
            nc.sync.dma_start(out=by_query(out[2 * pair + g])[:, ch, :], in_=res[u][:])

        nc.vector.tensor_copy(
            out=k_bf[:].rearrange("p r s j -> p s j r"),
            in_=k_raw[:].rearrange("p j (s r) -> p s j r", r=PACK),
        )
        for r in range(PACK):
            quantize(k_codes[0][:, r, 0:R], k_scales[0][:, r, 0:R], k_bf[:, r].rearrange("p s j -> p (s j)"))
        top, bottom = slice(0, R), slice(R, P)
        for dst, src in zip(k_window(0, top, 1), k_window(0, bottom, 0)):
            nc.sync.dma_start(out=dst, in_=src)
        for dst, src in zip(k_window(1, bottom, 0), k_window(0, top, 0)):
            nc.sync.dma_start(out=dst, in_=src)
        nc.sync.dma_start(out=v_raw[:], in_=v[0].rearrange("(p r) e -> p r e", r=PACK))
        load_q(1)
        nc.sync.dma_start(out=og_first[1][:], in_=by_query(og[1]))
        nc.sync.dma_start(
            out=og_last[:].rearrange("p h k x -> p h (k x)"), in_=og[2:4].rearrange("h (s c) e -> s h (c e)", c=4)
        )
        nc.vector.tensor_tensor(out=ratio[:], in0=inv0[:], in1=t_abs[:], op=ALU.mult)
        for dst, src in zip(k_window(1, bottom, 1), k_window(0, bottom, 0)):
            nc.vector.tensor_copy(out=dst, in_=src)
        interleave_q(0)
        dst, src = q_views(1)
        nc.scalar.copy(out=dst, in_=src)
        nc.vector.scalar_tensor_tensor(out=ln_t[:], in0=ratio[:], scalar=-1.0, in1=ln0[:], op0=ALU.add, op1=ALU.add)
        quantize_q(0)
        for u in range(2):
            scores(0, u)
            scores(1, u)
        tanh(0)
        quantize_q(1)
        nc.vector.tensor_tensor(
            out=v_bf[:].rearrange("p (a b) r -> p a r b", b=4),
            in0=v_raw[:].rearrange("p r (a b) -> p a r b", b=4),
            in1=t_sign[:].unsqueeze(1).unsqueeze(3).to_broadcast([P, E // 4, PACK, 4]),
            op=ALU.mult,
        )
        gate_on_vector(0)
        quantize(v_codes[:], v_scales[:], v_bf[:].rearrange("p e r -> p (e r)"))

        last = UNITS - 1
        gate_piece_at = {2: 1, 5: 2}
        for u in range(UNITS):
            exps(u, 0)
            ahead = 2 * (u // 2 + 1)
            if ahead < UNITS:
                scores(u % 2, ahead, ahead + 1)
            if u >= 1:
                values(u - 1)
            exps(u, 1)
            if u in gate_piece_at:
                tanh(gate_piece_at[u])
            if u == last:
                for g in range(2):
                    nc.scalar.activation(out=th[3][:, g], in_=og_piece[3][:, g], func=ACT.Tanh, scale=0.5)
                    nc.scalar.activation(out=gate[3][:, g], in_=th[3][:, g], func=ACT.Copy, scale=0.5, bias=0.5)
            interleave_w(u)
            if u < 2:
                interleave_q(2 + u)
            if u >= 2:
                finish(u - 2)
            if u == last:
                reciprocal(u - 1)
            quantize_w(u)
            if u < 2:
                quantize_q(2 + u)
            if 1 <= u < last:
                reciprocal(u - 1)
            if u in gate_piece_at:
                gate_on_vector(gate_piece_at[u])
        values(last)
        finish(last - 1)
        reciprocal(last)
        finish(last)
